import numpy as np
import ml_dtypes


def mxq(x, axis, fmt="e4m3"):
    dtype, down = {"e4m3": (ml_dtypes.float8_e4m3fn, 7), "e5m2": (ml_dtypes.float8_e5m2, 14)}[fmt]
    v = np.moveaxis(np.asarray(x, np.float32).astype(ml_dtypes.bfloat16).astype(np.float64), axis, -1)
    blocks = v.reshape(v.shape[:-1] + (-1, 32))
    amax = np.abs(blocks).max(-1, keepdims=True)
    byte = np.maximum(np.where(amax > 0, np.frexp(amax)[1] - 1 + 127, 0) - down, 1)
    scale = np.exp2(byte - 127.0)
    codes = (blocks / scale).astype(np.float32).astype(dtype).astype(np.float64)
    return np.moveaxis((codes * scale).reshape(v.shape), -1, axis)


WIDE = False


def mx_kscale(k):
    if not WIDE:
        return np.ones(k)
    levels = np.array([10, -10, 5, -5, 0])
    if k % 512:
        return np.exp2(np.random.permutation(np.resize(levels, k // 32))).repeat(32)
    a = np.empty((k // 512, 16))
    for p in range(k // 512):
        a[p, :8] = np.random.permutation(np.resize(levels, 8))
        for g in range(8):
            far = levels[np.abs(levels - a[p, g]) >= 10]
            a[p, g + 8] = far[np.random.randint(len(far))]
    return np.exp2(a.ravel()).repeat(32)


BF16 = ml_dtypes.bfloat16


def bf(x):
    return np.asarray(x, np.float32).astype(BF16)


def f64(x):
    return np.asarray(x).astype(np.float64)

E4M3FN = np.array([(-1.0 if i & 128 else 1.0) * ((1.0 + (i & 7) / 8.0) * 2.0 ** (((i >> 3) & 15) - 7) if i & 120 else (i & 7) * 2.0 ** -9) for i in range(256)])


def e4m3fn_bytes(y):
    return np.clip(np.asarray(y, np.float64), -448.0, 448.0).astype(np.float32).astype(ml_dtypes.float8_e4m3fn).view(np.uint8)


def e4m3fn_values(b):
    return E4M3FN[b]


T, D, R, N, B = 512, 2048, 1536, 3072, 128


def setup_inputs():
    s, t = mx_kscale(D), mx_kscale(R)
    w_dq = np.random.standard_normal((R, D)) / np.sqrt(D) / s
    w_uq = np.random.standard_normal((N, R)) / np.sqrt(R) / t
    w_dq_scale = (np.abs(w_dq).reshape(R // B, B, D // B, B).max(axis=(1, 3)) / 448).astype(np.float32)
    w_uq_scale = (np.abs(w_uq).reshape(N // B, B, R // B, B).max(axis=(1, 3)) / 448).astype(np.float32)
    return {"x": bf(np.random.standard_normal((T, D)) * s),
            "w_dq_bytes": e4m3fn_bytes(w_dq / np.repeat(np.repeat(f64(w_dq_scale), B, axis=0), B, axis=1)),
            "w_dq_scale": w_dq_scale,
            "b": bf(0.3 * np.random.standard_normal(R)),
            "g": bf((1 + 0.1 * np.random.standard_normal(R)) * t),
            "w_uq_bytes": e4m3fn_bytes(w_uq / np.repeat(np.repeat(f64(w_uq_scale), B, axis=0), B, axis=1)),
            "w_uq_scale": w_uq_scale}


def reference(x, w_dq_bytes, w_dq_scale, b, g, w_uq_bytes, w_uq_scale):
    w_dq = e4m3fn_values(w_dq_bytes) * np.repeat(np.repeat(f64(w_dq_scale), B, axis=0), B, axis=1)
    w_uq = e4m3fn_values(w_uq_bytes) * np.repeat(np.repeat(f64(w_uq_scale), B, axis=0), B, axis=1)
    z = mxq(f64(x), 1, "e4m3") @ mxq(w_dq, 1, "e4m3").T
    c = (z + f64(b)) * f64(g)
    return mxq(c, 1, "e4m3") @ mxq(w_uq, 1, "e4m3").T

@@ -1,0 +1,402 @@
+from contextlib import ExitStack
+
+import concourse.mybir as mybir
+from concourse.masks import make_identity
+
+F32 = mybir.dt.float32
+BF16 = mybir.dt.bfloat16
+U32 = mybir.dt.uint32
+U8 = mybir.dt.uint8
+FP8 = mybir.dt.float8_e4m3fn
+FP8X4 = mybir.dt.float8_e4m3fn_x4
+ACT = mybir.ActivationFunctionType
+ALU = mybir.AluOpType
+
+T, D, R, N, B = 512, 2048, 1536, 3072, 128
+P = 128
+KP = 512
+GD = D // KP
+GR = R // KP
+NA = R // P
+NB = N // 256
+FLOPS = 2 * T * D * R + 2 * T * R * N
+
+
+def turn_ahead(k):
+    return 2 if k < 9 else 1
+
+
+def EMPTY_LATE(k):
+    return False
+
+
+def ahead(k):
+    return 4 if k < 2 else 3 if k < 9 else 2
+
+
+S_PASSES = {4: (3,), 5: (3,), 6: (3,), 7: (3,), 8: (3,), 9: (3,), 10: (3,), 11: (3,)}
+
+
+def tile_mla_query_down_up_d5_kernel(tc, x, w_dq_bytes, w_dq_scale, b, g, w_uq_bytes, w_uq_scale, out):
+    nc = tc.nc
+    with ExitStack() as ctx:
+        keep = ctx.enter_context(tc.tile_pool(name="keep", bufs=1))
+        raws = ctx.enter_context(tc.tile_pool(name="raws", bufs=12))
+        xin = ctx.enter_context(tc.tile_pool(name="xin", bufs=4))
+        wids = ctx.enter_context(tc.tile_pool(name="wids", bufs=6))
+        grps = ctx.enter_context(tc.tile_pool(name="grps", bufs=3))
+        cods = ctx.enter_context(tc.tile_pool(name="cods", bufs=3))
+        cs = ctx.enter_context(tc.tile_pool(name="cs", bufs=2))
+        ckeep = ctx.enter_context(tc.tile_pool(name="ckeep", bufs=3))
+        ress = ctx.enter_context(tc.tile_pool(name="ress", bufs=6))
+        tps = ctx.enter_context(tc.psum_pool(name="tps", bufs=4))
+        accs = ctx.enter_context(tc.psum_pool(name="accs", bufs=4))
+
+        ident = keep.tile([P, P], F32)
+        make_identity(nc, ident[:])
+
+        ctx.enter_context(tc.manual_schedule())
+
+        sc_a = keep.tile([P, (R // B // 4) * (D // B)], F32)
+        sc_b = keep.tile([P, (N // B) * (R // B)], F32)
+        src = w_dq_scale.rearrange("(G s) j -> s G j", s=4)
+        for s in range(4):
+            nc.scalar.dma_start(
+                out=sc_a[32 * s : 32 * s + 32, :].rearrange("p (G j) -> p G j", j=D // B),
+                in_=src[s].partition_broadcast(32),
+            )
+        b_sb = keep.tile([P, NA], BF16)
+        g_sb = keep.tile([P, NA], BF16)
+        nc.scalar.dma_start(out=g_sb[:].rearrange("p (G t) -> p G t", t=4), in_=g.rearrange("(G m t) -> m G t", m=P, t=4))
+        nc.scalar.dma_start(out=b_sb[:].rearrange("p (G t) -> p G t", t=4), in_=b.rearrange("(G m t) -> m G t", m=P, t=4))
+        nc.scalar.dma_start(out=sc_b[:], in_=w_uq_scale.rearrange("i j -> (i j)").partition_broadcast(P))
+
+        raw_of = {}
+        x_of = []
+
+        def load_a(i):
+            raw_a = raws.tile([P, D], U8, align_bytes=64, bufs=8)
+            src = w_dq_bytes.rearrange("(G m t) k -> G t m k", m=P, t=4)[i // 4, i % 4]
+            pieces = 2 if i == 0 else 1
+            for n in range(pieces):
+                cols = slice(D // pieces * n, D // pieces * (n + 1))
+                nc.sync.dma_start(out=raw_a[:, cols], in_=src[:, cols])
+            raw_of[("A", i)] = raw_a
+
+        def load_b(h):
+            raw_b = raws.tile([P, 2 * R], U8, align_bytes=64, bufs=6)
+            nc.sync.dma_start(
+                out=raw_b[:].rearrange("p (r k) -> p r k", r=2),
+                in_=w_uq_bytes.rearrange("(h r p) k -> h p r k", r=2, p=P)[h],
+            )
+            raw_of[("B", h)] = raw_b
+
+        def load_x(tt):
+            x_sb = xin.tile([P, D], BF16, align_bytes=64)
+            nc.sync.dma_start(out=x_sb[:], in_=x[P * tt : P * (tt + 1), :])
+            x_of.append(x_sb)
+
+        order = [("A", i) for i in range(10)] + [("B", 0), ("B", 1), ("A", 10), ("A", 11)] + [("B", h) for h in range(2, NB - 2)] + [("L", ps) for ps in range(GR)]
+
+        load_a(0)
+        load_a(1)
+        load_x(0)
+        load_a(2)
+        load_x(1)
+        load_a(3)
+        load_x(2)
+        load_a(4)
+        load_x(3)
+        for kind, i in order[5:]:
+            if kind == "A":
+                load_a(i)
+            elif kind == "B":
+                load_b(i)
+        load_b(NB - 2)
+        load_b(NB - 1)
+
+        wid_of = {}
+        grp_of = {}
+        code_of = {}
+
+        def widen_block(dst, src8, scale, natural, q):
+            if natural:
+                nc.scalar.activation(out=dst[:, P * q : P * (q + 1)], in_=src8, func=ACT.Copy, scale=scale)
+            else:
+                nc.vector.tensor_scalar(
+                    out=dst.rearrange("r (u p e) -> r p u e", u=2, e=2)[:, 32 * q : 32 * q + 32],
+                    in0=src8,
+                    scalar1=scale,
+                    scalar2=None,
+                    op0=ALU.mult,
+                )
+
+        def widen(unit):
+            kind, i = unit
+            if kind == "L":
+                wid_l = wids.tile([P, 4 * KP], BF16, align_bytes=64, bufs=6, tag="wid_a")
+                wid_of[unit] = wid_l
+                for r in range(4):
+                    raw = raw_of[("B", NB - 2 + r // 2)]
+                    for q in range(4):
+                        j = 4 * i + q
+                        col = (2 * (NB - 2) + r) * (R // B) + j
+                        lo = R * (r % 2) + P * j
+                        widen_block(wid_l[:, KP * r : KP * (r + 1)], raw[:, lo : lo + P].bitcast(FP8), sc_b[:, col : col + 1], False, q)
+                return
+            raw = raw_of[unit]
+            if kind == "A":
+                wid_a = wids.tile([P, D], BF16, align_bytes=64, bufs=6)
+                wid_of[unit] = wid_a
+                for ps in range(GD):
+                    natural = ps in S_PASSES.get(i, ())
+                    for q in range(4):
+                        j = 4 * ps + q
+                        col = (i // 4) * (D // B) + j
+                        widen_block(wid_a[:, KP * ps : KP * (ps + 1)], raw[:, P * j : P * (j + 1)].bitcast(FP8), sc_a[:, col : col + 1], natural, q)
+            else:
+                wid_b = wids.tile([P, 2 * R], BF16, align_bytes=64, bufs=4)
+                wid_of[unit] = wid_b
+                for ps in range(GR):
+                    for r in range(2):
+                        for q in range(4):
+                            j = 4 * ps + q
+                            col = (2 * i + r) * (R // B) + j
+                            lo = R * r + KP * ps
+                            widen_block(wid_b[:, lo : lo + KP], raw[:, R * r + P * j : R * r + P * (j + 1)].bitcast(FP8), sc_b[:, col : col + 1], False, q)
+
+        def turn_piece(dst, words, lo, natural):
+            for u in range(2):
+                if natural:
+                    nc.tensor.transpose(dst[:, u, :], words[:, lo + u : lo + 256 : 2], ident[:])
+                else:
+                    nc.tensor.transpose(dst[:, u, :], words[:, lo + P * u : lo + P * (u + 1)], ident[:])
+
+        def turn(unit):
+            kind, i = unit
+            words = wid_of[unit][:].bitcast(F32)
+            if kind == "L":
+                grp_l = grps.tile([P, 512 * 4], BF16, align_bytes=64, bufs=4, tag="grp_a")
+                grp_of[unit] = grp_l
+                for half in range(2):
+                    pt = tps.tile([P, 2, 2, P], F32)
+                    for a in range(2):
+                        turn_piece(pt[:, a], words, 256 * (2 * half + a), False)
+                    dst = grp_l[:].bitcast(F32).rearrange("p (r n u) -> p r n u", r=4, u=2)[:, 2 * half : 2 * half + 2]
+                    if half == 1 and i == GR - 1:
+                        nc.vector.tensor_copy(out=dst, in_=pt[:].rearrange("p a u r -> p a r u"))
+                    else:
+                        nc.scalar.copy(out=dst, in_=pt[:].rearrange("p a u r -> p a r u"))
+            elif kind == "A":
+                grp_a = grps.tile([P, GD * P * 4], BF16, align_bytes=64, bufs=4)
+                grp_of[unit] = grp_a
+                gw = grp_a[:].bitcast(F32).rearrange("p (s m u) -> p s m u", s=GD, u=2)
+                for half in range(2):
+                    pt = tps.tile([P, 2, 2, P], F32)
+                    for a in range(2):
+                        ps = 2 * half + a
+                        turn_piece(pt[:, a], words, 256 * ps, ps in S_PASSES.get(i, ()))
+                    nc.scalar.copy(out=gw[:, 2 * half : 2 * half + 2], in_=pt[:].rearrange("p a u r -> p a r u"))
+            else:
+                if i % 2 == 0:
+                    grp_b = grps.tile([P, GR * 512 * 4], BF16, align_bytes=64, bufs=2)
+                    grp_of[("B", i // 2)] = grp_b
+                grp = grp_of[("B", i // 2)]
+                gw = grp[:].bitcast(F32).rearrange("p (s f u) -> p s f u", s=GR, u=2)
+                for ps in range(GR):
+                    pt = tps.tile([P, 2, 2, P], F32)
+                    for r in range(2):
+                        turn_piece(pt[:, r], words, (R // 2) * r + 256 * ps, False)
+                    lo = 256 * (i % 2)
+                    nc.scalar.copy(
+                        out=gw[:, ps, lo : lo + 256, :].rearrange("p (r n) u -> p r n u", r=2),
+                        in_=pt[:].rearrange("p a u r -> p a r u"),
+                    )
+
+        xg = keep.tile([P, GD * T * 4], BF16, align_bytes=64)
+        xq = keep.tile([P, GD * T], U32, align_bytes=64)
+        xs = keep.tile([P, GD * T], U8, align_bytes=64)
+        xw = xg[:].bitcast(F32).rearrange("p (s n u) -> p s n u", s=GD, u=2)
+
+        def turn_x(tt):
+            words = x_of[tt][:].bitcast(F32)
+            for half in range(2):
+                pt = tps.tile([P, 2, 2, P], F32)
+                for a in range(2):
+                    turn_piece(pt[:, a], words, 256 * (2 * half + a), True)
+                nc.scalar.copy(out=xw[:, 2 * half : 2 * half + 2, P * tt : P * (tt + 1), :], in_=pt[:].rearrange("p a u r -> p a r u"))
+
+        def quant(codes, scales, src_ap):
+            nc.vector.quantize_mx(out=codes.bitcast(FP8X4), scales=scales, in_=src_ap)
+
+        def quant_unit(unit):
+            kind, i = unit
+            if kind == "A":
+                cod_a = cods.tile([P, GD * P], U32, align_bytes=64)
+                scl_a = cods.tile([P, GD * P], U8, align_bytes=64)
+                quant(cod_a[:], scl_a[:], grp_of[unit][:])
+                code_of[unit] = (cod_a, scl_a)
+            elif kind == "L":
+                if i == 0:
+                    cod_b = cods.tile([P, GR * 512], U32, align_bytes=64)
+                    scl_b = cods.tile([P, GR * 512], U8, align_bytes=64)
+                    code_of[("B", NB // 2 - 1)] = (cod_b, scl_b)
+                cod_l, scl_l = code_of[("B", NB // 2 - 1)]
+                quant(cod_l[:, 512 * i : 512 * (i + 1)], scl_l[:, 512 * i : 512 * (i + 1)], grp_of[unit][:])
+            elif i % 2 == 1:
+                q = i // 2
+                cod_b = cods.tile([P, GR * 512], U32, align_bytes=64)
+                scl_b = cods.tile([P, GR * 512], U8, align_bytes=64)
+                for ps in range(GR):
+                    quant(cod_b[:, 512 * ps : 512 * (ps + 1)], scl_b[:, 512 * ps : 512 * (ps + 1)], grp_of[("B", q)][:, 2048 * ps : 2048 * (ps + 1)])
+                code_of[("B", q)] = (cod_b, scl_b)
+
+        g32 = keep.tile([P, NA], F32)
+        bg = keep.tile([P, NA], F32)
+
+        cp_of = {}
+        cg_of = {}
+        c_of = {}
+        acc_of = {}
+
+        def mm_a(i):
+            acc = accs.tile([P, T], F32)
+            acc_of[("A", i)] = acc
+            cod, scl = code_of[("A", i)]
+            for ps in range(GD):
+                nc.tensor.matmul_mx(
+                    out=acc[:],
+                    lhsT=cod[:, P * ps : P * (ps + 1)].bitcast(FP8X4),
+                    lhsT_scale=scl[:, P * ps : P * (ps + 1)],
+                    rhs=xq[:, T * ps : T * (ps + 1)].bitcast(FP8X4),
+                    rhs_scale=xs[:, T * ps : T * (ps + 1)],
+                    start=(ps == 0),
+                    stop=(ps == GD - 1),
+                )
+
+        def c_evac(i):
+            if i % 4 == 0:
+                cp = cs.tile([P, 4 * T], BF16, align_bytes=64)
+                cp_of[i // 4] = cp
+            nc.scalar.activation(
+                out=cp_of[i // 4][:, T * (i % 4) : T * (i % 4 + 1)],
+                in_=acc_of[("A", i)][:],
+                func=ACT.Identity,
+                bias=bg[:, i : i + 1],
+                scale=g32[:, i : i + 1],
+            )
+
+        def c_weave(G):
+            cg = cs.tile([P, 4 * T], BF16, align_bytes=64)
+            cg_of[G] = cg
+            nc.vector.tensor_copy(out=cg[:].rearrange("p (n t) -> p n t", t=4), in_=cp_of[G][:].rearrange("p (t n) -> p n t", t=4))
+
+        def c_quant(G):
+            c_cod = ckeep.tile([P, T], U32, align_bytes=64)
+            c_scl = ckeep.tile([P, T], U8, align_bytes=64)
+            quant(c_cod[:], c_scl[:], cg_of[G][:])
+            c_of[G] = (c_cod, c_scl)
+
+        def mm_b(q, passes, tts):
+            cod, scl = code_of[("B", q)]
+            for tt in tts:
+                if passes[0] == 0:
+                    acc = accs.tile([P, 512], F32)
+                    acc_of[("B", q, tt)] = acc
+                for ps in passes:
+                    c_cod, c_scl = c_of[ps]
+                    nc.tensor.matmul_mx(
+                        out=acc_of[("B", q, tt)][:],
+                        lhsT=c_cod[:, P * tt : P * (tt + 1)].bitcast(FP8X4),
+                        lhsT_scale=c_scl[:, P * tt : P * (tt + 1)],
+                        rhs=cod[:, 512 * ps : 512 * (ps + 1)].bitcast(FP8X4),
+                        rhs_scale=scl[:, 512 * ps : 512 * (ps + 1)],
+                        start=(ps == 0),
+                        stop=(ps == GR - 1),
+                    )
+
+        def out_evac(q, tt, on_vector):
+            res = ress.tile([P, 512], F32)
+            if on_vector:
+                nc.vector.tensor_copy(out=res[:], in_=acc_of[("B", q, tt)][:])
+            else:
+                nc.scalar.copy(out=res[:], in_=acc_of[("B", q, tt)][:])
+            nc.sync.dma_start(out=out[P * tt : P * (tt + 1), 512 * q : 512 * (q + 1)], in_=res[:])
+
+        widen(order[0])
+        widen(order[1])
+        turn_x(0)
+        widen(order[2])
+        turn(order[0])
+        turn_x(1)
+        widen(order[3])
+        turn_x(2)
+        turn_x(3)
+        widen(order[4])
+        nc.vector.tensor_copy(out=g32[:], in_=g_sb[:])
+        nc.vector.tensor_tensor(out=bg[:], in0=g_sb[:], in1=b_sb[:], op=ALU.mult)
+        for ps in range(GD):
+            quant(xq[:, T * ps : T * (ps + 1)], xs[:, T * ps : T * (ps + 1)], xg[:, 4 * T * ps : 4 * T * (ps + 1)])
+
+        wp = 5
+        tp = 1
+        pending = []
+        evacs = []
+        weave_at = {}
+        cquant_at = {}
+        steps = len(order)
+        last_q = NB // 2 - 1
+        for k in range(steps + 8):
+            jobs = evacs
+            evacs = []
+
+            def empty():
+                for job in jobs:
+                    if job[0] == "c":
+                        c_evac(job[1])
+                        if job[1] % 4 == 3:
+                            weave_at[k] = job[1] // 4
+                            cquant_at[k + 1] = job[1] // 4
+                    else:
+                        out_evac(job[1], job[2], job[1] == last_q and job[2] % 2 == 1)
+
+            if not EMPTY_LATE(k):
+                empty()
+            if k < steps:
+                quant_unit(order[k])
+                kind, i = order[k]
+                if kind == "L":
+                    pending.append((last_q, (i,), (0, 1, 2, 3)))
+                if kind == "B" and i % 2 == 1:
+                    q = i // 2
+                    if q == 0:
+                        pending.append((q, (0, 1), (0, 1, 2, 3)))
+                        pending.append((q, (2,), (0, 1, 2, 3)))
+                    else:
+                        pending.append((q, (0, 1, 2), (0, 1)))
+                        pending.append((q, (0, 1, 2), (2, 3)))
+            if k in cquant_at:
+                c_quant(cquant_at[k])
+            while tp < min(steps, k + 1 + turn_ahead(k)):
+                turn(order[tp])
+                tp += 1
+            if EMPTY_LATE(k):
+                empty()
+            if k < steps and order[k][0] == "A":
+                mm_a(order[k][1])
+                evacs.append(("c", order[k][1]))
+            budget = 2 if len(pending) > 2 else 1
+            if k >= steps:
+                budget = len(pending)
+            for n in range(budget):
+                if pending and k > order.index(("A", NA - 1)) and pending[0][1][-1] in c_of:
+                    q, passes, tts = pending.pop(0)
+                    mm_b(q, passes, tts)
+                    if passes[-1] == 2:
+                        for tt in tts:
+                            evacs.append(("o", q, tt))
+            while wp < min(steps, k + 1 + ahead(k)):
+                widen(order[wp])
+                wp += 1
+            if k in weave_at:
+                c_weave(weave_at[k])

@@ -12,391 +12,420 @@ FP8X4 = mybir.dt.float8_e4m3fn_x4
 ACT = mybir.ActivationFunctionType
 ALU = mybir.AluOpType
 
-T, D, R, N, B = 512, 2048, 1536, 3072, 128
+T, D, R, N = 512, 2048, 1536, 3072
 P = 128
-KP = 512
-GD = D // KP
-GR = R // KP
-NA = R // P
-NB = N // 256
+K_PASS = 512
+W_PASS = K_PASS // 2
+D_PASSES, R_PASSES = D // K_PASS, R // K_PASS
+TOKEN_TILES = T // P
+GROUP = 512
+LAST_GROUP = N // GROUP - 1
 FLOPS = 2 * T * D * R + 2 * T * R * N
 
+UNITS = (
+    [("dq", i) for i in range(10)]
+    + [("uq", 0), ("uq", 1), ("dq", 10), ("dq", 11)]
+    + [("uq", h) for h in range(2, 2 * LAST_GROUP)]
+    + [("end", r) for r in range(4)]
+)
 
-def turn_ahead(k):
-    return 2 if k < 9 else 1
+SCALAR_SHARE = dict(
+    [(("dq", i), ((2, 0),)) for i in (0, 1, 3, 5, 6, 7, 8, 11)]
+    + [(("uq", h), ((2, 1),)) for h in (0, 3)]
+    + [(("uq", h), ((1, 0), (2, 0), (2, 1))) for h in (1, 4)]
+)
+
+WIDEN_FIRST = 6
 
 
-def EMPTY_LATE(k):
-    return False
+def widened_by(step):
+    return step + 1 + (6 if step < 6 else 5 if step < 10 else 2 if step < 19 else 3)
 
 
-def ahead(k):
-    return 4 if k < 2 else 3 if k < 9 else 2
+def turned_by(step):
+    return step + 1 + (3 if step < 7 else 2 if step < 13 else 1 if step < 23 else 2)
 
 
-S_PASSES = {4: (3,), 5: (3,), 6: (3,), 7: (3,), 8: (3,), 9: (3,), 10: (3,), 11: (3,)}
+JOINED_STEP = 12
+
+ALL_PASSES = (0, 1, 2)
+PRODUCTS = {
+    14: ((0, (0, 1), (0, 1, 2, 3)),),
+    15: ((0, (2,), (0, 1, 2, 3)),),
+    16: ((1, ALL_PASSES, (0, 1)), (1, ALL_PASSES, (2, 3))),
+    17: ((2, ALL_PASSES, (0, 1)),),
+    18: ((2, ALL_PASSES, (2, 3)),),
+    19: ((3, ALL_PASSES, (0, 1)),),
+    20: ((3, ALL_PASSES, (2, 3)),),
+    22: ((4, ALL_PASSES, (0, 1)), (4, ALL_PASSES, (2, 3))),
+}
+END_PRODUCTS = {23: (0,), 24: (1,), 25: (2, 3)}
 
 
 def tile_mla_query_down_up_d5_kernel(tc, x, w_dq_bytes, w_dq_scale, b, g, w_uq_bytes, w_uq_scale, out):
     nc = tc.nc
     with ExitStack() as ctx:
         keep = ctx.enter_context(tc.tile_pool(name="keep", bufs=1))
-        raws = ctx.enter_context(tc.tile_pool(name="raws", bufs=12))
-        xin = ctx.enter_context(tc.tile_pool(name="xin", bufs=4))
-        wids = ctx.enter_context(tc.tile_pool(name="wids", bufs=6))
-        grps = ctx.enter_context(tc.tile_pool(name="grps", bufs=3))
-        cods = ctx.enter_context(tc.tile_pool(name="cods", bufs=3))
-        cs = ctx.enter_context(tc.tile_pool(name="cs", bufs=2))
-        ckeep = ctx.enter_context(tc.tile_pool(name="ckeep", bufs=3))
-        ress = ctx.enter_context(tc.tile_pool(name="ress", bufs=6))
-        tps = ctx.enter_context(tc.psum_pool(name="tps", bufs=4))
-        accs = ctx.enter_context(tc.psum_pool(name="accs", bufs=4))
+        raws = ctx.enter_context(tc.tile_pool(name="raws", bufs=8))
+        tokens = ctx.enter_context(tc.tile_pool(name="tokens", bufs=4))
+        wides = ctx.enter_context(tc.tile_pool(name="wides", bufs=8))
+        turneds = ctx.enter_context(tc.tile_pool(name="turneds", bufs=4))
+        codes = ctx.enter_context(tc.tile_pool(name="codes", bufs=3))
+        latents = ctx.enter_context(tc.tile_pool(name="latents", bufs=2))
+        latent_codes = ctx.enter_context(tc.tile_pool(name="latent_codes", bufs=3))
+        results = ctx.enter_context(tc.tile_pool(name="results", bufs=6))
+        turn_banks = ctx.enter_context(tc.psum_pool(name="turn_banks", bufs=4))
+        sum_banks = ctx.enter_context(tc.psum_pool(name="sum_banks", bufs=4))
 
         ident = keep.tile([P, P], F32)
         make_identity(nc, ident[:])
 
         ctx.enter_context(tc.manual_schedule())
 
-        sc_a = keep.tile([P, (R // B // 4) * (D // B)], F32)
-        sc_b = keep.tile([P, (N // B) * (R // B)], F32)
-        src = w_dq_scale.rearrange("(G s) j -> s G j", s=4)
+        dq_scale = keep.tile([P, (R // GROUP) * (D // P)], F32)
+        uq_scale = keep.tile([P, (N // P) * (R // P)], F32)
+        dq_scale_rows = w_dq_scale.rearrange("(G s) j -> s G j", s=4)
         for s in range(4):
             nc.scalar.dma_start(
-                out=sc_a[32 * s : 32 * s + 32, :].rearrange("p (G j) -> p G j", j=D // B),
-                in_=src[s].partition_broadcast(32),
+                out=dq_scale[32 * s : 32 * s + 32, :].rearrange("p (G j) -> p G j", j=D // P),
+                in_=dq_scale_rows[s].partition_broadcast(32),
             )
-        b_sb = keep.tile([P, NA], BF16)
-        g_sb = keep.tile([P, NA], BF16)
-        nc.scalar.dma_start(out=g_sb[:].rearrange("p (G t) -> p G t", t=4), in_=g.rearrange("(G m t) -> m G t", m=P, t=4))
-        nc.scalar.dma_start(out=b_sb[:].rearrange("p (G t) -> p G t", t=4), in_=b.rearrange("(G m t) -> m G t", m=P, t=4))
-        nc.scalar.dma_start(out=sc_b[:], in_=w_uq_scale.rearrange("i j -> (i j)").partition_broadcast(P))
+        b_raw = keep.tile([P, R // P], BF16)
+        g_raw = keep.tile([P, R // P], BF16)
+        for raw, vector in ((g_raw, g), (b_raw, b)):
+            nc.scalar.dma_start(
+                out=raw[:].rearrange("p (G t) -> p G t", t=4), in_=vector.rearrange("(G m t) -> m G t", m=P, t=4)
+            )
+        nc.scalar.dma_start(out=uq_scale[:], in_=w_uq_scale.rearrange("i j -> (i j)").partition_broadcast(P))
 
         raw_of = {}
         x_of = []
 
-        def load_a(i):
-            raw_a = raws.tile([P, D], U8, align_bytes=64, bufs=8)
-            src = w_dq_bytes.rearrange("(G m t) k -> G t m k", m=P, t=4)[i // 4, i % 4]
+        def load_dq(i):
+            dq_raw = raws.tile([P, D], U8, align_bytes=64)
+            rows = w_dq_bytes.rearrange("(G m t) k -> G t m k", m=P, t=4)[i // 4, i % 4]
             pieces = 2 if i == 0 else 1
             for n in range(pieces):
                 cols = slice(D // pieces * n, D // pieces * (n + 1))
-                nc.sync.dma_start(out=raw_a[:, cols], in_=src[:, cols])
-            raw_of[("A", i)] = raw_a
+                nc.sync.dma_start(out=dq_raw[:, cols], in_=rows[:, cols])
+            raw_of[("dq", i)] = dq_raw
 
-        def load_b(h):
-            raw_b = raws.tile([P, 2 * R], U8, align_bytes=64, bufs=6)
+        def load_uq(h):
+            uq_raw = raws.tile([P, 2 * R], U8, align_bytes=64, bufs=6)
             nc.sync.dma_start(
-                out=raw_b[:].rearrange("p (r k) -> p r k", r=2),
+                out=uq_raw[:].rearrange("p (r k) -> p r k", r=2),
                 in_=w_uq_bytes.rearrange("(h r p) k -> h p r k", r=2, p=P)[h],
             )
-            raw_of[("B", h)] = raw_b
+            raw_of[("uq", h)] = uq_raw
 
         def load_x(tt):
-            x_sb = xin.tile([P, D], BF16, align_bytes=64)
-            nc.sync.dma_start(out=x_sb[:], in_=x[P * tt : P * (tt + 1), :])
-            x_of.append(x_sb)
+            x_rows = tokens.tile([P, D], BF16, align_bytes=64)
+            nc.sync.dma_start(out=x_rows[:], in_=x[P * tt : P * (tt + 1), :])
+            x_of.append(x_rows)
 
-        order = [("A", i) for i in range(10)] + [("B", 0), ("B", 1), ("A", 10), ("A", 11)] + [("B", h) for h in range(2, NB - 2)] + [("L", ps) for ps in range(GR)]
+        load_dq(0)
+        load_dq(1)
+        for tt in range(TOKEN_TILES - 1):
+            load_x(tt)
+            load_dq(tt + 2)
+        load_x(TOKEN_TILES - 1)
+        for kind, i in UNITS[TOKEN_TILES + 1 :]:
+            if kind == "dq":
+                load_dq(i)
+            elif kind == "uq":
+                load_uq(i)
+        load_uq(2 * LAST_GROUP)
+        load_uq(2 * LAST_GROUP + 1)
 
-        load_a(0)
-        load_a(1)
-        load_x(0)
-        load_a(2)
-        load_x(1)
-        load_a(3)
-        load_x(2)
-        load_a(4)
-        load_x(3)
-        for kind, i in order[5:]:
-            if kind == "A":
-                load_a(i)
-            elif kind == "B":
-                load_b(i)
-        load_b(NB - 2)
-        load_b(NB - 1)
-
-        wid_of = {}
-        grp_of = {}
-        code_of = {}
-
-        def widen_block(dst, src8, scale, natural, q):
-            if natural:
-                nc.scalar.activation(out=dst[:, P * q : P * (q + 1)], in_=src8, func=ACT.Copy, scale=scale)
+        def bytes_of(unit, s, r, q):
+            kind, i = unit
+            j = 4 * s + q
+            if kind == "dq":
+                return raw_of[unit][:, P * j : P * (j + 1)], dq_scale[:, 16 * (i // 4) + j : 16 * (i // 4) + j + 1]
+            if kind == "uq":
+                raw, tile, lo = raw_of[unit], 2 * i + r, R * r
             else:
-                nc.vector.tensor_scalar(
-                    out=dst.rearrange("r (u p e) -> r p u e", u=2, e=2)[:, 32 * q : 32 * q + 32],
-                    in0=src8,
-                    scalar1=scale,
-                    scalar2=None,
-                    op0=ALU.mult,
-                )
+                raw, tile, lo = raw_of[("uq", 2 * LAST_GROUP + i // 2)], 4 * LAST_GROUP + i, R * (i % 2)
+            return raw[:, lo + P * j : lo + P * (j + 1)], uq_scale[:, 12 * tile + j : 12 * tile + j + 1]
+
+        wide_of = {}
+        turned_of = {}
+        codes_of = {}
+
+        def by_scalar(unit, s, r):
+            return (s, r) in SCALAR_SHARE.get(unit, ())
+
+        def widen_pass(unit, wide, s, r):
+            for q in range(4):
+                square, scale = bytes_of(unit, s, r, q)
+                if by_scalar(unit, s, r):
+                    nc.scalar.activation(out=wide[:, P * q : P * (q + 1)], in_=square.bitcast(FP8), func=ACT.Copy, scale=scale)
+                else:
+                    nc.vector.tensor_scalar(
+                        out=wide.rearrange("r (u p e) -> r p u e", u=2, e=2)[:, 32 * q : 32 * q + 32],
+                        in0=square.bitcast(FP8),
+                        scalar1=scale,
+                        scalar2=None,
+                        op0=ALU.mult,
+                    )
 
         def widen(unit):
             kind, i = unit
-            if kind == "L":
-                wid_l = wids.tile([P, 4 * KP], BF16, align_bytes=64, bufs=6, tag="wid_a")
-                wid_of[unit] = wid_l
-                for r in range(4):
-                    raw = raw_of[("B", NB - 2 + r // 2)]
-                    for q in range(4):
-                        j = 4 * i + q
-                        col = (2 * (NB - 2) + r) * (R // B) + j
-                        lo = R * (r % 2) + P * j
-                        widen_block(wid_l[:, KP * r : KP * (r + 1)], raw[:, lo : lo + P].bitcast(FP8), sc_b[:, col : col + 1], False, q)
-                return
-            raw = raw_of[unit]
-            if kind == "A":
-                wid_a = wids.tile([P, D], BF16, align_bytes=64, bufs=6)
-                wid_of[unit] = wid_a
-                for ps in range(GD):
-                    natural = ps in S_PASSES.get(i, ())
-                    for q in range(4):
-                        j = 4 * ps + q
-                        col = (i // 4) * (D // B) + j
-                        widen_block(wid_a[:, KP * ps : KP * (ps + 1)], raw[:, P * j : P * (j + 1)].bitcast(FP8), sc_a[:, col : col + 1], natural, q)
-            else:
-                wid_b = wids.tile([P, 2 * R], BF16, align_bytes=64, bufs=4)
-                wid_of[unit] = wid_b
-                for ps in range(GR):
+            if kind == "uq":
+                wide_pair = wides.tile([P, 2 * R], BF16, align_bytes=64, bufs=4)
+                wide_of[unit] = wide_pair
+                for s in range(R_PASSES):
                     for r in range(2):
-                        for q in range(4):
-                            j = 4 * ps + q
-                            col = (2 * i + r) * (R // B) + j
-                            lo = R * r + KP * ps
-                            widen_block(wid_b[:, lo : lo + KP], raw[:, R * r + P * j : R * r + P * (j + 1)].bitcast(FP8), sc_b[:, col : col + 1], False, q)
+                        lo = R * r + K_PASS * s
+                        widen_pass(unit, wide_pair[:, lo : lo + K_PASS], s, r)
+            else:
+                length = D if kind == "dq" else R
+                wide_tile = wides.tile([P, length], BF16, align_bytes=64)
+                wide_of[unit] = wide_tile
+                for s in range(length // K_PASS):
+                    widen_pass(unit, wide_tile[:, K_PASS * s : K_PASS * (s + 1)], s, 0)
 
-        def turn_piece(dst, words, lo, natural):
+        def turn_pass(bank, words, lo, as_it_lies):
             for u in range(2):
-                if natural:
-                    nc.tensor.transpose(dst[:, u, :], words[:, lo + u : lo + 256 : 2], ident[:])
+                if as_it_lies:
+                    nc.tensor.transpose(bank[:, u, :], words[:, lo + u : lo + W_PASS : 2], ident[:])
                 else:
-                    nc.tensor.transpose(dst[:, u, :], words[:, lo + P * u : lo + P * (u + 1)], ident[:])
+                    nc.tensor.transpose(bank[:, u, :], words[:, lo + P * u : lo + P * (u + 1)], ident[:])
+
+        def empty_turned(dst, bank):
+            nc.scalar.copy(out=dst, in_=bank.rearrange("p a u r -> p a r u"))
 
         def turn(unit):
             kind, i = unit
-            words = wid_of[unit][:].bitcast(F32)
-            if kind == "L":
-                grp_l = grps.tile([P, 512 * 4], BF16, align_bytes=64, bufs=4, tag="grp_a")
-                grp_of[unit] = grp_l
-                for half in range(2):
-                    pt = tps.tile([P, 2, 2, P], F32)
-                    for a in range(2):
-                        turn_piece(pt[:, a], words, 256 * (2 * half + a), False)
-                    dst = grp_l[:].bitcast(F32).rearrange("p (r n u) -> p r n u", r=4, u=2)[:, 2 * half : 2 * half + 2]
-                    if half == 1 and i == GR - 1:
-                        nc.vector.tensor_copy(out=dst, in_=pt[:].rearrange("p a u r -> p a r u"))
-                    else:
-                        nc.scalar.copy(out=dst, in_=pt[:].rearrange("p a u r -> p a r u"))
-            elif kind == "A":
-                grp_a = grps.tile([P, GD * P * 4], BF16, align_bytes=64, bufs=4)
-                grp_of[unit] = grp_a
-                gw = grp_a[:].bitcast(F32).rearrange("p (s m u) -> p s m u", s=GD, u=2)
-                for half in range(2):
-                    pt = tps.tile([P, 2, 2, P], F32)
-                    for a in range(2):
-                        ps = 2 * half + a
-                        turn_piece(pt[:, a], words, 256 * ps, ps in S_PASSES.get(i, ()))
-                    nc.scalar.copy(out=gw[:, 2 * half : 2 * half + 2], in_=pt[:].rearrange("p a u r -> p a r u"))
-            else:
+            words = wide_of[unit][:].bitcast(F32)
+            if kind == "uq":
                 if i % 2 == 0:
-                    grp_b = grps.tile([P, GR * 512 * 4], BF16, align_bytes=64, bufs=2)
-                    grp_of[("B", i // 2)] = grp_b
-                grp = grp_of[("B", i // 2)]
-                gw = grp[:].bitcast(F32).rearrange("p (s f u) -> p s f u", s=GR, u=2)
-                for ps in range(GR):
-                    pt = tps.tile([P, 2, 2, P], F32)
+                    turned_group = turneds.tile([P, R_PASSES * GROUP * 4], BF16, align_bytes=64, bufs=2)
+                    turned_of[i // 2] = turned_group
+                dst = turned_of[i // 2][:].bitcast(F32).rearrange("p (s f u) -> p s f u", s=R_PASSES, u=2)
+                lo = 256 * (i % 2)
+                for s in range(R_PASSES):
+                    bank = turn_banks.tile([P, 2, 2, P], F32)
                     for r in range(2):
-                        turn_piece(pt[:, r], words, (R // 2) * r + 256 * ps, False)
-                    lo = 256 * (i % 2)
-                    nc.scalar.copy(
-                        out=gw[:, ps, lo : lo + 256, :].rearrange("p (r n) u -> p r n u", r=2),
-                        in_=pt[:].rearrange("p a u r -> p a r u"),
-                    )
+                        turn_pass(bank[:, r], words, R // 2 * r + W_PASS * s, by_scalar(unit, s, r))
+                    empty_turned(dst[:, s, lo : lo + 256, :].rearrange("p (r n) u -> p r n u", r=2), bank[:])
+            else:
+                passes = D_PASSES if kind == "dq" else R_PASSES
+                turned_tile = turneds.tile([P, passes * P * 4], BF16, align_bytes=64)
+                turned_of[unit] = turned_tile
+                dst = turned_tile[:].bitcast(F32).rearrange("p (s m u) -> p s m u", s=passes, u=2)
+                for first in range(0, passes, 2):
+                    many = min(2, passes - first)
+                    bank = turn_banks.tile([P, 2, 2, P], F32)
+                    for a in range(many):
+                        turn_pass(bank[:, a], words, W_PASS * (first + a), by_scalar(unit, first + a, 0))
+                    empty_turned(dst[:, first : first + many], bank[:, :many])
 
-        xg = keep.tile([P, GD * T * 4], BF16, align_bytes=64)
-        xq = keep.tile([P, GD * T], U32, align_bytes=64)
-        xs = keep.tile([P, GD * T], U8, align_bytes=64)
-        xw = xg[:].bitcast(F32).rearrange("p (s n u) -> p s n u", s=GD, u=2)
+        x_turned = keep.tile([P, D_PASSES * T * 4], BF16, align_bytes=64)
+        x_codes = keep.tile([P, D_PASSES * T], U32, align_bytes=64)
+        x_scales = keep.tile([P, D_PASSES * T], U8, align_bytes=64)
 
         def turn_x(tt):
             words = x_of[tt][:].bitcast(F32)
-            for half in range(2):
-                pt = tps.tile([P, 2, 2, P], F32)
+            dst = x_turned[:].bitcast(F32).rearrange("p (s n u) -> p s n u", s=D_PASSES, u=2)
+            for first in range(0, D_PASSES, 2):
+                bank = turn_banks.tile([P, 2, 2, P], F32)
                 for a in range(2):
-                    turn_piece(pt[:, a], words, 256 * (2 * half + a), True)
-                nc.scalar.copy(out=xw[:, 2 * half : 2 * half + 2, P * tt : P * (tt + 1), :], in_=pt[:].rearrange("p a u r -> p a r u"))
+                    turn_pass(bank[:, a], words, W_PASS * (first + a), True)
+                empty_turned(dst[:, first : first + 2, P * tt : P * (tt + 1), :], bank[:])
 
-        def quant(codes, scales, src_ap):
-            nc.vector.quantize_mx(out=codes.bitcast(FP8X4), scales=scales, in_=src_ap)
+        def quantise(code, scale, source):
+            nc.vector.quantize_mx(out=code.bitcast(FP8X4), scales=scale, in_=source)
 
-        def quant_unit(unit):
+        def quantise_unit(unit):
             kind, i = unit
-            if kind == "A":
-                cod_a = cods.tile([P, GD * P], U32, align_bytes=64)
-                scl_a = cods.tile([P, GD * P], U8, align_bytes=64)
-                quant(cod_a[:], scl_a[:], grp_of[unit][:])
-                code_of[unit] = (cod_a, scl_a)
-            elif kind == "L":
-                if i == 0:
-                    cod_b = cods.tile([P, GR * 512], U32, align_bytes=64)
-                    scl_b = cods.tile([P, GR * 512], U8, align_bytes=64)
-                    code_of[("B", NB // 2 - 1)] = (cod_b, scl_b)
-                cod_l, scl_l = code_of[("B", NB // 2 - 1)]
-                quant(cod_l[:, 512 * i : 512 * (i + 1)], scl_l[:, 512 * i : 512 * (i + 1)], grp_of[unit][:])
+            if kind == "dq":
+                tile_codes = codes.tile([P, K_PASS], U32, align_bytes=64)
+                tile_scales = codes.tile([P, K_PASS], U8, align_bytes=64)
+                quantise(tile_codes[:], tile_scales[:], turned_of[unit][:])
+                codes_of[unit] = (tile_codes, tile_scales)
+            elif kind == "end":
+                tile_codes = codes.tile([P, R_PASSES * P], U32, align_bytes=64)
+                tile_scales = codes.tile([P, R_PASSES * P], U8, align_bytes=64)
+                for s in range(R_PASSES):
+                    cols = slice(P * s, P * (s + 1))
+                    quantise(tile_codes[:, cols], tile_scales[:, cols], turned_of[unit][:, 4 * P * s : 4 * P * (s + 1)])
+                codes_of[unit] = (tile_codes, tile_scales)
             elif i % 2 == 1:
-                q = i // 2
-                cod_b = cods.tile([P, GR * 512], U32, align_bytes=64)
-                scl_b = cods.tile([P, GR * 512], U8, align_bytes=64)
-                for ps in range(GR):
-                    quant(cod_b[:, 512 * ps : 512 * (ps + 1)], scl_b[:, 512 * ps : 512 * (ps + 1)], grp_of[("B", q)][:, 2048 * ps : 2048 * (ps + 1)])
-                code_of[("B", q)] = (cod_b, scl_b)
+                group_codes = codes.tile([P, R_PASSES * GROUP], U32, align_bytes=64, bufs=2)
+                group_scales = codes.tile([P, R_PASSES * GROUP], U8, align_bytes=64, bufs=2)
+                for s in range(R_PASSES):
+                    cols = slice(GROUP * s, GROUP * (s + 1))
+                    quantise(
+                        group_codes[:, cols],
+                        group_scales[:, cols],
+                        turned_of[i // 2][:, 4 * GROUP * s : 4 * GROUP * (s + 1)],
+                    )
+                codes_of[i // 2] = (group_codes, group_scales)
 
-        g32 = keep.tile([P, NA], F32)
-        bg = keep.tile([P, NA], F32)
-
-        cp_of = {}
-        cg_of = {}
-        c_of = {}
-        acc_of = {}
-
-        def mm_a(i):
-            acc = accs.tile([P, T], F32)
-            acc_of[("A", i)] = acc
-            cod, scl = code_of[("A", i)]
-            for ps in range(GD):
-                nc.tensor.matmul_mx(
-                    out=acc[:],
-                    lhsT=cod[:, P * ps : P * (ps + 1)].bitcast(FP8X4),
-                    lhsT_scale=scl[:, P * ps : P * (ps + 1)],
-                    rhs=xq[:, T * ps : T * (ps + 1)].bitcast(FP8X4),
-                    rhs_scale=xs[:, T * ps : T * (ps + 1)],
-                    start=(ps == 0),
-                    stop=(ps == GD - 1),
-                )
-
-        def c_evac(i):
-            if i % 4 == 0:
-                cp = cs.tile([P, 4 * T], BF16, align_bytes=64)
-                cp_of[i // 4] = cp
-            nc.scalar.activation(
-                out=cp_of[i // 4][:, T * (i % 4) : T * (i % 4 + 1)],
-                in_=acc_of[("A", i)][:],
-                func=ACT.Identity,
-                bias=bg[:, i : i + 1],
-                scale=g32[:, i : i + 1],
+        def mx(bank, stationary, stationary_cols, moving, moving_cols, first, last):
+            nc.tensor.matmul_mx(
+                out=bank,
+                lhsT=stationary[0][:, stationary_cols].bitcast(FP8X4),
+                lhsT_scale=stationary[1][:, stationary_cols],
+                rhs=moving[0][:, moving_cols].bitcast(FP8X4),
+                rhs_scale=moving[1][:, moving_cols],
+                start=first,
+                stop=last,
             )
 
-        def c_weave(G):
-            cg = cs.tile([P, 4 * T], BF16, align_bytes=64)
-            cg_of[G] = cg
-            nc.vector.tensor_copy(out=cg[:].rearrange("p (n t) -> p n t", t=4), in_=cp_of[G][:].rearrange("p (t n) -> p n t", t=4))
+        gain = keep.tile([P, R // P], F32)
+        bias_gain = keep.tile([P, R // P], F32)
 
-        def c_quant(G):
-            c_cod = ckeep.tile([P, T], U32, align_bytes=64)
-            c_scl = ckeep.tile([P, T], U8, align_bytes=64)
-            quant(c_cod[:], c_scl[:], cg_of[G][:])
-            c_of[G] = (c_cod, c_scl)
+        sums_of = {}
+        planes_of = {}
+        woven_of = {}
+        c_of = {}
 
-        def mm_b(q, passes, tts):
-            cod, scl = code_of[("B", q)]
-            for tt in tts:
+        def first_product(i):
+            sums = sum_banks.tile([P, T], F32)
+            sums_of[("dq", i)] = sums
+            for s in range(D_PASSES):
+                mx(
+                    sums[:],
+                    codes_of[("dq", i)],
+                    slice(P * s, P * (s + 1)),
+                    (x_codes, x_scales),
+                    slice(T * s, T * (s + 1)),
+                    s == 0,
+                    s == D_PASSES - 1,
+                )
+
+        def empty_latents(i):
+            G, t = i // 4, i % 4
+            if t == 0:
+                planes = latents.tile([P, 4 * T], BF16, align_bytes=64)
+                planes_of[G] = planes
+            nc.scalar.activation(
+                out=planes_of[G][:, T * t : T * (t + 1)],
+                in_=sums_of[("dq", i)][:],
+                func=ACT.Identity,
+                bias=bias_gain[:, i : i + 1],
+                scale=gain[:, i : i + 1],
+            )
+
+        def weave_latents(G):
+            woven = latents.tile([P, 4 * T], BF16, align_bytes=64)
+            woven_of[G] = woven
+            nc.vector.tensor_copy(
+                out=woven[:].rearrange("p (n t) -> p n t", t=4), in_=planes_of[G][:].rearrange("p (t n) -> p n t", t=4)
+            )
+
+        def quantise_latents(G):
+            c_codes = latent_codes.tile([P, T], U32, align_bytes=64)
+            c_scales = latent_codes.tile([P, T], U8, align_bytes=64)
+            quantise(c_codes[:], c_scales[:], woven_of[G][:])
+            c_of[G] = (c_codes, c_scales)
+
+        def second_product(group, passes, token_tiles):
+            for tt in token_tiles:
                 if passes[0] == 0:
-                    acc = accs.tile([P, 512], F32)
-                    acc_of[("B", q, tt)] = acc
-                for ps in passes:
-                    c_cod, c_scl = c_of[ps]
-                    nc.tensor.matmul_mx(
-                        out=acc_of[("B", q, tt)][:],
-                        lhsT=c_cod[:, P * tt : P * (tt + 1)].bitcast(FP8X4),
-                        lhsT_scale=c_scl[:, P * tt : P * (tt + 1)],
-                        rhs=cod[:, 512 * ps : 512 * (ps + 1)].bitcast(FP8X4),
-                        rhs_scale=scl[:, 512 * ps : 512 * (ps + 1)],
-                        start=(ps == 0),
-                        stop=(ps == GR - 1),
+                    sums = sum_banks.tile([P, GROUP], F32)
+                    sums_of[(group, tt)] = sums
+                for s in passes:
+                    mx(
+                        sums_of[(group, tt)][:],
+                        c_of[s],
+                        slice(P * tt, P * (tt + 1)),
+                        codes_of[group],
+                        slice(GROUP * s, GROUP * (s + 1)),
+                        s == 0,
+                        s == R_PASSES - 1,
                     )
 
-        def out_evac(q, tt, on_vector):
-            res = ress.tile([P, 512], F32)
-            if on_vector:
-                nc.vector.tensor_copy(out=res[:], in_=acc_of[("B", q, tt)][:])
-            else:
-                nc.scalar.copy(out=res[:], in_=acc_of[("B", q, tt)][:])
-            nc.sync.dma_start(out=out[P * tt : P * (tt + 1), 512 * q : 512 * (q + 1)], in_=res[:])
+        def end_product(r):
+            sums = sum_banks.tile([P, TOKEN_TILES * P], F32)
+            sums_of[("end", r)] = sums
+            for tt in range(TOKEN_TILES):
+                for s in range(R_PASSES):
+                    mx(
+                        sums[:, P * tt : P * (tt + 1)],
+                        c_of[s],
+                        slice(P * tt, P * (tt + 1)),
+                        codes_of[("end", r)],
+                        slice(P * s, P * (s + 1)),
+                        s == 0,
+                        s == R_PASSES - 1,
+                    )
 
-        widen(order[0])
-        widen(order[1])
+        def empty_group(group, tt):
+            result = results.tile([P, GROUP], F32)
+            nc.scalar.copy(out=result[:], in_=sums_of[(group, tt)][:])
+            nc.sync.dma_start(out=out[P * tt : P * (tt + 1), GROUP * group : GROUP * (group + 1)], in_=result[:])
+
+        def empty_end(r):
+            f0 = GROUP * LAST_GROUP + P * r
+            result = results.tile([P, TOKEN_TILES * P], F32)
+            for half in range(2):
+                cols = slice(2 * P * half, 2 * P * (half + 1))
+                copy = nc.vector.tensor_copy if (r, half) == (3, 1) else nc.scalar.copy
+                copy(out=result[:, cols], in_=sums_of[("end", r)][:, cols])
+                nc.sync.dma_start(
+                    out=out[2 * P * half : 2 * P * (half + 1), f0 : f0 + P].rearrange("(t p) f -> p t f", p=P),
+                    in_=result[:, cols].rearrange("p (t f) -> p t f", t=2),
+                )
+
+        widen(UNITS[0])
+        widen(UNITS[1])
         turn_x(0)
-        widen(order[2])
-        turn(order[0])
+        widen(UNITS[2])
+        turn(UNITS[0])
         turn_x(1)
-        widen(order[3])
+        widen(UNITS[3])
         turn_x(2)
         turn_x(3)
-        widen(order[4])
-        nc.vector.tensor_copy(out=g32[:], in_=g_sb[:])
-        nc.vector.tensor_tensor(out=bg[:], in0=g_sb[:], in1=b_sb[:], op=ALU.mult)
-        for ps in range(GD):
-            quant(xq[:, T * ps : T * (ps + 1)], xs[:, T * ps : T * (ps + 1)], xg[:, 4 * T * ps : 4 * T * (ps + 1)])
+        widen(UNITS[4])
+        widen(UNITS[5])
+        nc.vector.tensor_copy(out=gain[:], in_=g_raw[:])
+        nc.vector.tensor_tensor(out=bias_gain[:], in0=g_raw[:], in1=b_raw[:], op=ALU.mult)
+        for s in range(D_PASSES):
+            cols = slice(T * s, T * (s + 1))
+            quantise(x_codes[:, cols], x_scales[:, cols], x_turned[:, 4 * T * s : 4 * T * (s + 1)])
+        widened, turned = WIDEN_FIRST, 1
 
-        wp = 5
-        tp = 1
-        pending = []
-        evacs = []
-        weave_at = {}
-        cquant_at = {}
-        steps = len(order)
-        last_q = NB // 2 - 1
-        for k in range(steps + 8):
-            jobs = evacs
-            evacs = []
+        to_multiply = []
+        to_empty = []
+        to_quantise = []
+        for step in range(len(UNITS) + 1):
+            to_weave = []
+            for empty, args in to_empty:
+                empty(*args)
+                if empty == empty_latents and args[0] % 4 == 3:
+                    to_weave.append(args[0] // 4)
+            to_empty = []
 
-            def empty():
-                for job in jobs:
-                    if job[0] == "c":
-                        c_evac(job[1])
-                        if job[1] % 4 == 3:
-                            weave_at[k] = job[1] // 4
-                            cquant_at[k + 1] = job[1] // 4
-                    else:
-                        out_evac(job[1], job[2], job[1] == last_q and job[2] % 2 == 1)
+            if step < len(UNITS):
+                quantise_unit(UNITS[step])
+                if UNITS[step][0] == "dq":
+                    to_multiply.append(UNITS[step][1])
+            for G in to_quantise:
+                quantise_latents(G)
+            to_quantise = to_weave
 
-            if not EMPTY_LATE(k):
-                empty()
-            if k < steps:
-                quant_unit(order[k])
-                kind, i = order[k]
-                if kind == "L":
-                    pending.append((last_q, (i,), (0, 1, 2, 3)))
-                if kind == "B" and i % 2 == 1:
-                    q = i // 2
-                    if q == 0:
-                        pending.append((q, (0, 1), (0, 1, 2, 3)))
-                        pending.append((q, (2,), (0, 1, 2, 3)))
-                    else:
-                        pending.append((q, (0, 1, 2), (0, 1)))
-                        pending.append((q, (0, 1, 2), (2, 3)))
-            if k in cquant_at:
-                c_quant(cquant_at[k])
-            while tp < min(steps, k + 1 + turn_ahead(k)):
-                turn(order[tp])
-                tp += 1
-            if EMPTY_LATE(k):
-                empty()
-            if k < steps and order[k][0] == "A":
-                mm_a(order[k][1])
-                evacs.append(("c", order[k][1]))
-            budget = 2 if len(pending) > 2 else 1
-            if k >= steps:
-                budget = len(pending)
-            for n in range(budget):
-                if pending and k > order.index(("A", NA - 1)) and pending[0][1][-1] in c_of:
-                    q, passes, tts = pending.pop(0)
-                    mm_b(q, passes, tts)
-                    if passes[-1] == 2:
-                        for tt in tts:
-                            evacs.append(("o", q, tt))
-            while wp < min(steps, k + 1 + ahead(k)):
-                widen(order[wp])
-                wp += 1
-            if k in weave_at:
-                c_weave(weave_at[k])
+            if step != JOINED_STEP:
+                while turned < min(len(UNITS), turned_by(step)):
+                    turn(UNITS[turned])
+                    turned += 1
+                for i in to_multiply:
+                    first_product(i)
+                    to_empty.append((empty_latents, (i,)))
+                to_multiply = []
+                for group, passes, token_tiles in PRODUCTS.get(step, ()):
+                    second_product(group, passes, token_tiles)
+                    if passes[-1] == R_PASSES - 1:
+                        for tt in token_tiles:
+                            to_empty.append((empty_group, (group, tt)))
+                for r in END_PRODUCTS.get(step, ()):
+                    end_product(r)
+                    to_empty.append((empty_end, (r,)))
+
+            while widened < min(len(UNITS), widened_by(step)):
+                widen(UNITS[widened])
+                widened += 1
+            for G in to_weave:
+                weave_latents(G)

from contextlib import ExitStack

import concourse.mybir as mybir
from concourse.masks import make_identity

F32 = mybir.dt.float32
BF16 = mybir.dt.bfloat16
U32 = mybir.dt.uint32
U8 = mybir.dt.uint8
FP8 = mybir.dt.float8_e4m3fn
FP8X4 = mybir.dt.float8_e4m3fn_x4
ACT = mybir.ActivationFunctionType
ALU = mybir.AluOpType

T, D, R, N = 512, 2048, 1536, 3072
P = 128
K_PASS = 512
W_PASS = K_PASS // 2
D_PASSES, R_PASSES = D // K_PASS, R // K_PASS
TOKEN_TILES = T // P
GROUP = 512
LAST_GROUP = N // GROUP - 1
FLOPS = 2 * T * D * R + 2 * T * R * N

UNITS = (
    [("dq", i) for i in range(10)]
    + [("uq", 0), ("uq", 1), ("dq", 10), ("dq", 11)]
    + [("uq", h) for h in range(2, 2 * LAST_GROUP)]
    + [("end", r) for r in range(4)]
)

SCALAR_SHARE = dict(
    [(("dq", i), ((2, 0),)) for i in (0, 1, 3, 5, 6, 7, 8, 11)]
    + [(("uq", h), ((2, 1),)) for h in (0, 3)]
    + [(("uq", h), ((1, 0), (2, 0), (2, 1))) for h in (1, 4)]
)

WIDEN_FIRST = 6


def widened_by(step):
    return step + 1 + (6 if step < 6 else 5 if step < 10 else 2 if step < 19 else 3)


def turned_by(step):
    return step + 1 + (3 if step < 7 else 2 if step < 13 else 1 if step < 23 else 2)


JOINED_STEP = 12

ALL_PASSES = (0, 1, 2)
PRODUCTS = {
    14: ((0, (0, 1), (0, 1, 2, 3)),),
    15: ((0, (2,), (0, 1, 2, 3)),),
    16: ((1, ALL_PASSES, (0, 1)), (1, ALL_PASSES, (2, 3))),
    17: ((2, ALL_PASSES, (0, 1)),),
    18: ((2, ALL_PASSES, (2, 3)),),
    19: ((3, ALL_PASSES, (0, 1)),),
    20: ((3, ALL_PASSES, (2, 3)),),
    22: ((4, ALL_PASSES, (0, 1)), (4, ALL_PASSES, (2, 3))),
}
END_PRODUCTS = {23: (0,), 24: (1,), 25: (2, 3)}


def tile_mla_query_down_up_d5_kernel(tc, x, w_dq_bytes, w_dq_scale, b, g, w_uq_bytes, w_uq_scale, out):
    nc = tc.nc
    with ExitStack() as ctx:
        keep = ctx.enter_context(tc.tile_pool(name="keep", bufs=1))
        raws = ctx.enter_context(tc.tile_pool(name="raws", bufs=8))
        tokens = ctx.enter_context(tc.tile_pool(name="tokens", bufs=4))
        wides = ctx.enter_context(tc.tile_pool(name="wides", bufs=8))
        turneds = ctx.enter_context(tc.tile_pool(name="turneds", bufs=4))
        codes = ctx.enter_context(tc.tile_pool(name="codes", bufs=3))
        latents = ctx.enter_context(tc.tile_pool(name="latents", bufs=2))
        latent_codes = ctx.enter_context(tc.tile_pool(name="latent_codes", bufs=3))
        results = ctx.enter_context(tc.tile_pool(name="results", bufs=6))
        turn_banks = ctx.enter_context(tc.psum_pool(name="turn_banks", bufs=4))
        sum_banks = ctx.enter_context(tc.psum_pool(name="sum_banks", bufs=4))

        ident = keep.tile([P, P], F32)
        make_identity(nc, ident[:])

        ctx.enter_context(tc.manual_schedule())

        dq_scale = keep.tile([P, (R // GROUP) * (D // P)], F32)
        uq_scale = keep.tile([P, (N // P) * (R // P)], F32)
        dq_scale_rows = w_dq_scale.rearrange("(G s) j -> s G j", s=4)
        for s in range(4):
            nc.scalar.dma_start(
                out=dq_scale[32 * s : 32 * s + 32, :].rearrange("p (G j) -> p G j", j=D // P),
                in_=dq_scale_rows[s].partition_broadcast(32),
            )
        b_raw = keep.tile([P, R // P], BF16)
        g_raw = keep.tile([P, R // P], BF16)
        for raw, vector in ((g_raw, g), (b_raw, b)):
            nc.scalar.dma_start(
                out=raw[:].rearrange("p (G t) -> p G t", t=4), in_=vector.rearrange("(G m t) -> m G t", m=P, t=4)
            )
        nc.scalar.dma_start(out=uq_scale[:], in_=w_uq_scale.rearrange("i j -> (i j)").partition_broadcast(P))

        raw_of = {}
        x_of = []

        def load_dq(i):
            dq_raw = raws.tile([P, D], U8, align_bytes=64)
            rows = w_dq_bytes.rearrange("(G m t) k -> G t m k", m=P, t=4)[i // 4, i % 4]
            pieces = 2 if i == 0 else 1
            for n in range(pieces):
                cols = slice(D // pieces * n, D // pieces * (n + 1))
                nc.sync.dma_start(out=dq_raw[:, cols], in_=rows[:, cols])
            raw_of[("dq", i)] = dq_raw

        def load_uq(h):
            uq_raw = raws.tile([P, 2 * R], U8, align_bytes=64, bufs=6)
            nc.sync.dma_start(
                out=uq_raw[:].rearrange("p (r k) -> p r k", r=2),
                in_=w_uq_bytes.rearrange("(h r p) k -> h p r k", r=2, p=P)[h],
            )
            raw_of[("uq", h)] = uq_raw

        def load_x(tt):
            x_rows = tokens.tile([P, D], BF16, align_bytes=64)
            nc.sync.dma_start(out=x_rows[:], in_=x[P * tt : P * (tt + 1), :])
            x_of.append(x_rows)

        load_dq(0)
        load_dq(1)
        for tt in range(TOKEN_TILES - 1):
            load_x(tt)
            load_dq(tt + 2)
        load_x(TOKEN_TILES - 1)
        for kind, i in UNITS[TOKEN_TILES + 1 :]:
            if kind == "dq":
                load_dq(i)
            elif kind == "uq":
                load_uq(i)
        load_uq(2 * LAST_GROUP)
        load_uq(2 * LAST_GROUP + 1)

        def bytes_of(unit, s, r, q):
            kind, i = unit
            j = 4 * s + q
            if kind == "dq":
                return raw_of[unit][:, P * j : P * (j + 1)], dq_scale[:, 16 * (i // 4) + j : 16 * (i // 4) + j + 1]
            if kind == "uq":
                raw, tile, lo = raw_of[unit], 2 * i + r, R * r
            else:
                raw, tile, lo = raw_of[("uq", 2 * LAST_GROUP + i // 2)], 4 * LAST_GROUP + i, R * (i % 2)
            return raw[:, lo + P * j : lo + P * (j + 1)], uq_scale[:, 12 * tile + j : 12 * tile + j + 1]

        wide_of = {}
        turned_of = {}
        codes_of = {}

        def by_scalar(unit, s, r):
            return (s, r) in SCALAR_SHARE.get(unit, ())

        def widen_pass(unit, wide, s, r):
            for q in range(4):
                square, scale = bytes_of(unit, s, r, q)
                if by_scalar(unit, s, r):
                    nc.scalar.activation(out=wide[:, P * q : P * (q + 1)], in_=square.bitcast(FP8), func=ACT.Copy, scale=scale)
                else:
                    nc.vector.tensor_scalar(
                        out=wide.rearrange("r (u p e) -> r p u e", u=2, e=2)[:, 32 * q : 32 * q + 32],
                        in0=square.bitcast(FP8),
                        scalar1=scale,
                        scalar2=None,
                        op0=ALU.mult,
                    )

        def widen(unit):
            kind, i = unit
            if kind == "uq":
                wide_pair = wides.tile([P, 2 * R], BF16, align_bytes=64, bufs=4)
                wide_of[unit] = wide_pair
                for s in range(R_PASSES):
                    for r in range(2):
                        lo = R * r + K_PASS * s
                        widen_pass(unit, wide_pair[:, lo : lo + K_PASS], s, r)
            else:
                length = D if kind == "dq" else R
                wide_tile = wides.tile([P, length], BF16, align_bytes=64)
                wide_of[unit] = wide_tile
                for s in range(length // K_PASS):
                    widen_pass(unit, wide_tile[:, K_PASS * s : K_PASS * (s + 1)], s, 0)

        def turn_pass(bank, words, lo, as_it_lies):
            for u in range(2):
                if as_it_lies:
                    nc.tensor.transpose(bank[:, u, :], words[:, lo + u : lo + W_PASS : 2], ident[:])
                else:
                    nc.tensor.transpose(bank[:, u, :], words[:, lo + P * u : lo + P * (u + 1)], ident[:])

        def empty_turned(dst, bank):
            nc.scalar.copy(out=dst, in_=bank.rearrange("p a u r -> p a r u"))

        def turn(unit):
            kind, i = unit
            words = wide_of[unit][:].bitcast(F32)
            if kind == "uq":
                if i % 2 == 0:
                    turned_group = turneds.tile([P, R_PASSES * GROUP * 4], BF16, align_bytes=64, bufs=2)
                    turned_of[i // 2] = turned_group
                dst = turned_of[i // 2][:].bitcast(F32).rearrange("p (s f u) -> p s f u", s=R_PASSES, u=2)
                lo = 256 * (i % 2)
                for s in range(R_PASSES):
                    bank = turn_banks.tile([P, 2, 2, P], F32)
                    for r in range(2):
                        turn_pass(bank[:, r], words, R // 2 * r + W_PASS * s, by_scalar(unit, s, r))
                    empty_turned(dst[:, s, lo : lo + 256, :].rearrange("p (r n) u -> p r n u", r=2), bank[:])
            else:
                passes = D_PASSES if kind == "dq" else R_PASSES
                turned_tile = turneds.tile([P, passes * P * 4], BF16, align_bytes=64)
                turned_of[unit] = turned_tile
                dst = turned_tile[:].bitcast(F32).rearrange("p (s m u) -> p s m u", s=passes, u=2)
                for first in range(0, passes, 2):
                    many = min(2, passes - first)
                    bank = turn_banks.tile([P, 2, 2, P], F32)
                    for a in range(many):
                        turn_pass(bank[:, a], words, W_PASS * (first + a), by_scalar(unit, first + a, 0))
                    empty_turned(dst[:, first : first + many], bank[:, :many])

        x_turned = keep.tile([P, D_PASSES * T * 4], BF16, align_bytes=64)
        x_codes = keep.tile([P, D_PASSES * T], U32, align_bytes=64)
        x_scales = keep.tile([P, D_PASSES * T], U8, align_bytes=64)

        def turn_x(tt):
            words = x_of[tt][:].bitcast(F32)
            dst = x_turned[:].bitcast(F32).rearrange("p (s n u) -> p s n u", s=D_PASSES, u=2)
            for first in range(0, D_PASSES, 2):
                bank = turn_banks.tile([P, 2, 2, P], F32)
                for a in range(2):
                    turn_pass(bank[:, a], words, W_PASS * (first + a), True)
                empty_turned(dst[:, first : first + 2, P * tt : P * (tt + 1), :], bank[:])

        def quantise(code, scale, source):
            nc.vector.quantize_mx(out=code.bitcast(FP8X4), scales=scale, in_=source)

        def quantise_unit(unit):
            kind, i = unit
            if kind == "dq":
                tile_codes = codes.tile([P, K_PASS], U32, align_bytes=64)
                tile_scales = codes.tile([P, K_PASS], U8, align_bytes=64)
                quantise(tile_codes[:], tile_scales[:], turned_of[unit][:])
                codes_of[unit] = (tile_codes, tile_scales)
            elif kind == "end":
                tile_codes = codes.tile([P, R_PASSES * P], U32, align_bytes=64)
                tile_scales = codes.tile([P, R_PASSES * P], U8, align_bytes=64)
                for s in range(R_PASSES):
                    cols = slice(P * s, P * (s + 1))
                    quantise(tile_codes[:, cols], tile_scales[:, cols], turned_of[unit][:, 4 * P * s : 4 * P * (s + 1)])
                codes_of[unit] = (tile_codes, tile_scales)
            elif i % 2 == 1:
                group_codes = codes.tile([P, R_PASSES * GROUP], U32, align_bytes=64, bufs=2)
                group_scales = codes.tile([P, R_PASSES * GROUP], U8, align_bytes=64, bufs=2)
                for s in range(R_PASSES):
                    cols = slice(GROUP * s, GROUP * (s + 1))
                    quantise(
                        group_codes[:, cols],
                        group_scales[:, cols],
                        turned_of[i // 2][:, 4 * GROUP * s : 4 * GROUP * (s + 1)],
                    )
                codes_of[i // 2] = (group_codes, group_scales)

        def mx(bank, stationary, stationary_cols, moving, moving_cols, first, last):
            nc.tensor.matmul_mx(
                out=bank,
                lhsT=stationary[0][:, stationary_cols].bitcast(FP8X4),
                lhsT_scale=stationary[1][:, stationary_cols],
                rhs=moving[0][:, moving_cols].bitcast(FP8X4),
                rhs_scale=moving[1][:, moving_cols],
                start=first,
                stop=last,
            )

        gain = keep.tile([P, R // P], F32)
        bias_gain = keep.tile([P, R // P], F32)

        sums_of = {}
        planes_of = {}
        woven_of = {}
        c_of = {}

        def first_product(i):
            sums = sum_banks.tile([P, T], F32)
            sums_of[("dq", i)] = sums
            for s in range(D_PASSES):
                mx(
                    sums[:],
                    codes_of[("dq", i)],
                    slice(P * s, P * (s + 1)),
                    (x_codes, x_scales),
                    slice(T * s, T * (s + 1)),
                    s == 0,
                    s == D_PASSES - 1,
                )

        def empty_latents(i):
            G, t = i // 4, i % 4
            if t == 0:
                planes = latents.tile([P, 4 * T], BF16, align_bytes=64)
                planes_of[G] = planes
            nc.scalar.activation(
                out=planes_of[G][:, T * t : T * (t + 1)],
                in_=sums_of[("dq", i)][:],
                func=ACT.Identity,
                bias=bias_gain[:, i : i + 1],
                scale=gain[:, i : i + 1],
            )

        def weave_latents(G):
            woven = latents.tile([P, 4 * T], BF16, align_bytes=64)
            woven_of[G] = woven
            nc.vector.tensor_copy(
                out=woven[:].rearrange("p (n t) -> p n t", t=4), in_=planes_of[G][:].rearrange("p (t n) -> p n t", t=4)
            )

        def quantise_latents(G):
            c_codes = latent_codes.tile([P, T], U32, align_bytes=64)
            c_scales = latent_codes.tile([P, T], U8, align_bytes=64)
            quantise(c_codes[:], c_scales[:], woven_of[G][:])
            c_of[G] = (c_codes, c_scales)

        def second_product(group, passes, token_tiles):
            for tt in token_tiles:
                if passes[0] == 0:
                    sums = sum_banks.tile([P, GROUP], F32)
                    sums_of[(group, tt)] = sums
                for s in passes:
                    mx(
                        sums_of[(group, tt)][:],
                        c_of[s],
                        slice(P * tt, P * (tt + 1)),
                        codes_of[group],
                        slice(GROUP * s, GROUP * (s + 1)),
                        s == 0,
                        s == R_PASSES - 1,
                    )

        def end_product(r):
            sums = sum_banks.tile([P, TOKEN_TILES * P], F32)
            sums_of[("end", r)] = sums
            for tt in range(TOKEN_TILES):
                for s in range(R_PASSES):
                    mx(
                        sums[:, P * tt : P * (tt + 1)],
                        c_of[s],
                        slice(P * tt, P * (tt + 1)),
                        codes_of[("end", r)],
                        slice(P * s, P * (s + 1)),
                        s == 0,
                        s == R_PASSES - 1,
                    )

        def empty_group(group, tt):
            result = results.tile([P, GROUP], F32)
            nc.scalar.copy(out=result[:], in_=sums_of[(group, tt)][:])
            nc.sync.dma_start(out=out[P * tt : P * (tt + 1), GROUP * group : GROUP * (group + 1)], in_=result[:])

        def empty_end(r):
            f0 = GROUP * LAST_GROUP + P * r
            result = results.tile([P, TOKEN_TILES * P], F32)
            for half in range(2):
                cols = slice(2 * P * half, 2 * P * (half + 1))
                copy = nc.vector.tensor_copy if (r, half) == (3, 1) else nc.scalar.copy
                copy(out=result[:, cols], in_=sums_of[("end", r)][:, cols])
                nc.sync.dma_start(
                    out=out[2 * P * half : 2 * P * (half + 1), f0 : f0 + P].rearrange("(t p) f -> p t f", p=P),
                    in_=result[:, cols].rearrange("p (t f) -> p t f", t=2),
                )

        widen(UNITS[0])
        widen(UNITS[1])
        turn_x(0)
        widen(UNITS[2])
        turn(UNITS[0])
        turn_x(1)
        widen(UNITS[3])
        turn_x(2)
        turn_x(3)
        widen(UNITS[4])
        widen(UNITS[5])
        nc.vector.tensor_copy(out=gain[:], in_=g_raw[:])
        nc.vector.tensor_tensor(out=bias_gain[:], in0=g_raw[:], in1=b_raw[:], op=ALU.mult)
        for s in range(D_PASSES):
            cols = slice(T * s, T * (s + 1))
            quantise(x_codes[:, cols], x_scales[:, cols], x_turned[:, 4 * T * s : 4 * T * (s + 1)])
        widened, turned = WIDEN_FIRST, 1

        to_multiply = []
        to_empty = []
        to_quantise = []
        for step in range(len(UNITS) + 1):
            to_weave = []
            for empty, args in to_empty:
                empty(*args)
                if empty == empty_latents and args[0] % 4 == 3:
                    to_weave.append(args[0] // 4)
            to_empty = []

            if step < len(UNITS):
                quantise_unit(UNITS[step])
                if UNITS[step][0] == "dq":
                    to_multiply.append(UNITS[step][1])
            for G in to_quantise:
                quantise_latents(G)
            to_quantise = to_weave

            if step != JOINED_STEP:
                while turned < min(len(UNITS), turned_by(step)):
                    turn(UNITS[turned])
                    turned += 1
                for i in to_multiply:
                    first_product(i)
                    to_empty.append((empty_latents, (i,)))
                to_multiply = []
                for group, passes, token_tiles in PRODUCTS.get(step, ()):
                    second_product(group, passes, token_tiles)
                    if passes[-1] == R_PASSES - 1:
                        for tt in token_tiles:
                            to_empty.append((empty_group, (group, tt)))
                for r in END_PRODUCTS.get(step, ()):
                    end_product(r)
                    to_empty.append((empty_end, (r,)))

            while widened < min(len(UNITS), widened_by(step)):
                widen(UNITS[widened])
                widened += 1
            for G in to_weave:
                weave_latents(G)
